import numpy as np
import ml_dtypes

BF16 = ml_dtypes.bfloat16


def bf(x):
    return np.asarray(x, np.float32).astype(BF16)


def f32(x):
    return np.asarray(x, np.float32)


def f64(x):
    return np.asarray(x).astype(np.float64)


def striped(idx):
    return np.concatenate([l.reshape(-1, 16).T for l in idx])


def rows(idx, k):
    return np.tile(np.repeat(idx, 16, axis=0), (k // (16 * 8), 1))


def look(tab, idx):
    return np.take_along_axis(f64(tab), rows(idx, len(tab)), axis=1)


K, S, V, N = 256, 2048, 2048, 2048


def setup_inputs():
    return {"tab": f32(np.random.standard_normal((2, K, S))), "y": f32(1.0 * np.random.standard_normal((K, V))), "offs": striped(np.stack([np.random.permutation(S)[:N] for _ in range(8)]))}


def reference(tab, y, offs):
    idx = np.stack([g.T.reshape(-1) for g in np.split(offs, 8)])
    x = look(tab[0], idx) / (1.0 + np.exp(-look(tab[0], idx))) * f64(y) + look(tab[1], idx)
    return x

@@ -1,0 +1,57 @@
+import concourse.mybir as mybir
+
+F32 = mybir.dt.float32
+U16 = mybir.dt.uint16
+ADD = mybir.AluOpType.add
+MULT = mybir.AluOpType.mult
+SILU = mybir.ActivationFunctionType.Silu
+
+P = 128
+PIECE = 512
+ENTRIES_PER_COLUMN = 16
+
+
+def tile_lookup_resglu_out_kernel(tc, tab, y, offs, out):
+    nc = tc.nc
+    rows, places = tab.shape[1], tab.shape[2]
+    entries = y.shape[1]
+    half = entries // 2
+    blocks = rows // P
+
+    with (
+        tc.tile_pool(name="held", bufs=1) as held,
+        tc.tile_pool(name="pieces", bufs=blocks * (entries // PIECE)) as pieces,
+    ):
+        offsets = held.tile([P, entries // ENTRIES_PER_COLUMN], U16, name="offsets")
+        nc.sync.dma_start(offsets[:], offs)
+
+        gates, shifts, streams = [], [], []
+        for b in range(blocks):
+            block_rows = slice(b * P, (b + 1) * P)
+            gate = held.tile([P, places], F32, name=f"gate{b}")
+            shift = held.tile([P, places], F32, name=f"shift{b}")
+            stream = held.tile([P, entries], F32, name=f"stream{b}")
+            nc.sync.dma_start(gate[:], tab[0, block_rows, :])
+            nc.sync.dma_start(stream[:, 0:half], y[block_rows, 0:half])
+            nc.sync.dma_start(shift[:], tab[1, block_rows, :])
+            nc.sync.dma_start(stream[:, half:entries], y[block_rows, half:entries])
+            gates.append(gate)
+            shifts.append(shift)
+            streams.append(stream)
+
+        for b in range(blocks):
+            block_rows = slice(b * P, (b + 1) * P)
+            for start in range(0, entries, PIECE):
+                piece = slice(start, start + PIECE)
+                listed = offsets[:, start // ENTRIES_PER_COLUMN : (start + PIECE) // ENTRIES_PER_COLUMN]
+
+                opened = pieces.tile([P, PIECE], F32, name="opened")
+                nc.scalar.activation(opened[:], gates[b][:].indirect(listed), SILU)
+
+                gated = pieces.tile([P, PIECE], F32, name="gated")
+                nc.vector.tensor_tensor(gated[:], opened[:], streams[b][:, piece], MULT)
+
+                result = pieces.tile([P, PIECE], F32, name="result")
+                nc.vector.tensor_tensor(result[:], shifts[b][:].indirect(listed), gated[:], ADD)
+
+                nc.sync.dma_start(out[block_rows, piece], result[:])

@@ -25,6 +25,11 @@ def tile_lookup_resglu_out_kernel(tc, tab, y, offs, out):
         offsets = held.tile([P, entries // ENTRIES_PER_COLUMN], U16, name="offsets")
         nc.sync.dma_start(offsets[:], offs)
 
+        zero = held.tile([P, 1], F32, name="zero")
+        nc.vector.memset(zero[:], 0.0)
+        warmed = held.tile([P, 1], F32, name="warmed")
+        nc.scalar.activation(warmed[:], zero[:], SILU)
+
         gates, shifts, streams = [], [], []
         for b in range(blocks):
             block_rows = slice(b * P, (b + 1) * P)

import concourse.mybir as mybir

F32 = mybir.dt.float32
U16 = mybir.dt.uint16
ADD = mybir.AluOpType.add
MULT = mybir.AluOpType.mult
SILU = mybir.ActivationFunctionType.Silu

P = 128
PIECE = 512
ENTRIES_PER_COLUMN = 16


def tile_lookup_resglu_out_kernel(tc, tab, y, offs, out):
    nc = tc.nc
    rows, places = tab.shape[1], tab.shape[2]
    entries = y.shape[1]
    half = entries // 2
    blocks = rows // P

    with (
        tc.tile_pool(name="held", bufs=1) as held,
        tc.tile_pool(name="pieces", bufs=blocks * (entries // PIECE)) as pieces,
    ):
        offsets = held.tile([P, entries // ENTRIES_PER_COLUMN], U16, name="offsets")
        nc.sync.dma_start(offsets[:], offs)

        zero = held.tile([P, 1], F32, name="zero")
        nc.vector.memset(zero[:], 0.0)
        warmed = held.tile([P, 1], F32, name="warmed")
        nc.scalar.activation(warmed[:], zero[:], SILU)

        gates, shifts, streams = [], [], []
        for b in range(blocks):
            block_rows = slice(b * P, (b + 1) * P)
            gate = held.tile([P, places], F32, name=f"gate{b}")
            shift = held.tile([P, places], F32, name=f"shift{b}")
            stream = held.tile([P, entries], F32, name=f"stream{b}")
            nc.sync.dma_start(gate[:], tab[0, block_rows, :])
            nc.sync.dma_start(stream[:, 0:half], y[block_rows, 0:half])
            nc.sync.dma_start(shift[:], tab[1, block_rows, :])
            nc.sync.dma_start(stream[:, half:entries], y[block_rows, half:entries])
            gates.append(gate)
            shifts.append(shift)
            streams.append(stream)

        for b in range(blocks):
            block_rows = slice(b * P, (b + 1) * P)
            for start in range(0, entries, PIECE):
                piece = slice(start, start + PIECE)
                listed = offsets[:, start // ENTRIES_PER_COLUMN : (start + PIECE) // ENTRIES_PER_COLUMN]

                opened = pieces.tile([P, PIECE], F32, name="opened")
                nc.scalar.activation(opened[:], gates[b][:].indirect(listed), SILU)

                gated = pieces.tile([P, PIECE], F32, name="gated")
                nc.vector.tensor_tensor(gated[:], opened[:], streams[b][:, piece], MULT)

                result = pieces.tile([P, PIECE], F32, name="result")
                nc.vector.tensor_tensor(result[:], shifts[b][:].indirect(listed), gated[:], ADD)

                nc.sync.dma_start(out[block_rows, piece], result[:])
